import numpy as np
import ml_dtypes


def mxq(x, axis, fmt="e4m3"):
    dtype, down = {"e4m3": (ml_dtypes.float8_e4m3fn, 7), "e5m2": (ml_dtypes.float8_e5m2, 14)}[fmt]
    v = np.moveaxis(np.asarray(x, np.float32).astype(ml_dtypes.bfloat16).astype(np.float64), axis, -1)
    blocks = v.reshape(v.shape[:-1] + (-1, 32))
    amax = np.abs(blocks).max(-1, keepdims=True)
    byte = np.maximum(np.where(amax > 0, np.frexp(amax)[1] - 1 + 127, 0) - down, 1)
    scale = np.exp2(byte - 127.0)
    codes = (blocks / scale).astype(np.float32).astype(dtype).astype(np.float64)
    return np.moveaxis((codes * scale).reshape(v.shape), -1, axis)


WIDE = False


def mx_kscale(k):
    if not WIDE:
        return np.ones(k)
    levels = np.array([24, -24, 12, -12, 0])
    if k % 512:
        return np.exp2(np.random.permutation(np.resize(levels, k // 32))).repeat(32)
    a = np.empty((k // 512, 16))
    for p in range(k // 512):
        a[p, :8] = np.random.permutation(np.resize(levels, 8))
        for g in range(8):
            far = levels[np.abs(levels - a[p, g]) >= 10]
            a[p, g + 8] = far[np.random.randint(len(far))]
    return np.exp2(a.ravel()).repeat(32)


def f64(x):
    return np.asarray(x).astype(np.float64)


def striped8(idx):
    return np.concatenate([v.reshape(-1, 16).T for v in idx]).astype(np.uint16)


def unstriped8(offs):
    return np.stack([offs[16 * g:16 * g + 16].T.reshape(-1) for g in range(8)]).astype(np.int64)


E2M1 = np.array([0.0, 0.5, 1.0, 1.5, 2.0, 3.0, 4.0, 6.0, -0.0, -0.5, -1.0, -1.5, -2.0, -3.0, -4.0, -6.0])


def pack_weight(w, fmt):
    k, n = w.shape
    w = f64(np.asarray(w, np.float32).astype(ml_dtypes.bfloat16)).reshape(k // 32, 32, n)
    amax = np.abs(w).max(1)
    if fmt == "e4m3":
        byte = np.frexp(amax)[1] - 1 + 127 - 7
    else:
        mant, ex = np.frexp(amax / 6.0)
        byte = np.where(mant > 0.5, ex, ex - 1) + 127
    byte = np.clip(np.where(amax > 0, byte, 1), 1, 254)
    scaled = (w * np.exp2(127.0 - byte)[:, None, :]).reshape(k, n).astype(np.float32)
    by_word = np.ascontiguousarray(scaled.reshape(k // 512, 128, 4, n).transpose(0, 1, 3, 2))
    if fmt == "e4m3":
        words = by_word.astype(ml_dtypes.float8_e4m3fn).view(np.uint8)
    else:
        c = by_word.astype(ml_dtypes.float4_e2m1fn).view(np.uint8) & 0xF
        words = (c[..., 0::2] | (c[..., 1::2] << 4)).reshape(k // 512, 128, 2 * n)
    return np.ascontiguousarray(words), np.ascontiguousarray(byte.astype(np.uint8).reshape(k // 512, 16, n))


def unpack_weight(words, scales, fmt):
    g, _, n = scales.shape
    words = np.ascontiguousarray(words).reshape(g, 128, n, -1)
    if fmt == "e4m3":
        vals = words.view(ml_dtypes.float8_e4m3fn).astype(np.float64)
    else:
        nib = np.empty((g, 128, n, 4), np.uint8)
        nib[..., 0::2] = words & 0xF
        nib[..., 1::2] = words >> 4
        vals = E2M1[nib]
    vals = vals * np.repeat(np.exp2(scales.astype(np.float64) - 127.0), 8, axis=1)[..., None]
    return vals.transpose(0, 1, 3, 2).reshape(g * 512, n)


def split(x):
    m, e = np.frexp(f64(x))
    hi = np.ldexp(np.trunc(16.0 * m) / 16.0, e)
    return hi, f64(x) - hi


def sigm(f):
    return 1.0 / (1.0 + np.exp(-np.maximum(f, -700.0)))


K, N, T, J = 1024, 512, 2048, 1024


def setup_inputs():
    n = np.random.standard_normal
    s = mx_kscale(K)[:, None]
    p_wv = pack_weight(n((K, N)) / np.sqrt(K) / s, "e4m3")
    return {
        "xT": (n((K, T)) * s).astype(np.float32),
        "wgt": np.repeat(np.random.uniform(0.5, 2.0, (8, J)), 16, axis=0).astype(np.float32),
        "wk": (n((K, N)) / np.sqrt(K) / s).astype(np.float32),
        "wv_words": p_wv[0],
        "wv_scales": p_wv[1],
        "bg": (0.3 * n(N) - 1.0).astype(np.float32),
        "res": (n((N, J))).astype(np.float32),
        "wgo": np.repeat(np.random.uniform(0.5, 2.0, (8, J)), 16, axis=0).astype(np.float32),
        "offs": striped8(np.stack([np.random.permutation(T)[:J] for _ in range(8)])),
        "offs2": striped8(np.stack([np.random.permutation(T)[:J] for _ in range(8)])),
    }


def reference(xT, wgt, wk, wv_words, wv_scales, bg, res, wgo, offs, offs2):
    idx = unstriped8(offs)
    idx2 = unstriped8(offs2)
    rows = np.arange(K)
    xg = f64(wgt)[rows // 4 % 128] * f64(xT)[rows[:, None], idx[rows % 512 // 64]]
    xT_ = mxq(xg, 0, "e4m3")
    wk_hi, wk_lo = split(wk)
    wk_hi_, wk_lo_ = mxq(wk_hi, 0, "e4m3"), mxq(wk_lo, 0, "e4m3")
    wv_ = unpack_weight(wv_words, wv_scales, "e4m3")
    ke = wk_hi_.T @ xT_ + wk_lo_.T @ xT_
    ve = wv_.T @ xT_
    gate = sigm(ke + f64(bg)[:, None])
    out = np.zeros((N, T))
    rows = np.arange(N)
    out[rows[:, None], idx2[rows % 128 // 16]] = f64(wgo)[rows % 128] * (f64(res) + gate * (ve - f64(res)))
    return out

@@ -1,0 +1,252 @@
+from contextlib import ExitStack
+
+import concourse.mybir as mybir
+from concourse.masks import make_identity
+
+K, N, T, J = 1024, 512, 2048, 1024
+FLOPS = 3 * 2 * K * N * J
+
+F32 = mybir.dt.float32
+BF16 = mybir.dt.bfloat16
+I32 = mybir.dt.int32
+U32 = mybir.dt.uint32
+U16 = mybir.dt.uint16
+U8 = mybir.dt.uint8
+FP8X4 = mybir.dt.float8_e4m3fn_x4
+ALU = mybir.AluOpType
+ACT = mybir.ActivationFunctionType
+
+P = 128
+PACK = 4
+PASSES = K // (P * PACK)
+JH = 512
+HALVES = J // JH
+NT = N // P
+LIST_COLS = JH // 16
+HI_MASK = 0xFFF0FFF0 - (1 << 32)
+
+
+def tile_list_hl_hwayS_kernel(
+    tc, xT, wgt, wk, wv_words, wv_scales, bg, res, wgo, offs, offs2, out
+):
+    nc = tc.nc
+    with ExitStack() as ctx:
+        keep = ctx.enter_context(tc.tile_pool(name="keep", bufs=1))
+        ring = ctx.enter_context(tc.tile_pool(name="ring", bufs=1))
+        psum = ctx.enter_context(tc.psum_pool(name="psum", bufs=1))
+
+        offs_t = keep.tile([P, J // 16], U16, name="offs_t")
+        offs2_t = keep.tile([P, J // 16], U16, name="offs2_t")
+        wgt_t = keep.tile([P, J], F32, name="wgt_t")
+        wgo_t = keep.tile([P, J], F32, name="wgo_t")
+        bg_t = keep.tile([P, NT], F32, name="bg_t")
+        wv_codes = keep.tile([P, PASSES, N], U32, name="wv_codes", align_bytes=64)
+        wv_sc = keep.tile([P, PASSES, N], U8, name="wv_sc", align_bytes=64)
+
+        x_rows = xT.rearrange("(a p i) t -> a i p t", a=PASSES, i=PACK)
+        wk_rows = wk.rearrange("(a p i) n -> a p i n", a=PASSES, i=PACK)
+
+        ident = keep.tile([P, P], F32, name="ident")
+        make_identity(nc, ident[:])
+        nc.vector.memset(wv_sc[:].bitcast(I32), 0)
+        windows = []
+        for nt in range(2):
+            w = keep.tile([P, T], F32, name=f"win{nt}")
+            nc.vector.memset(w[:], 0.0)
+            windows.append(w)
+
+        wk_raw = {}
+        wk_q = {}
+
+        def load_wk(a, n0, n1):
+            raw = keep.tile([P, PACK, n1 - n0], F32, name=f"wk_raw_{a}_{n0}")
+            nc.sync.dma_start(raw[:], wk_rows[a][:, :, n0:n1])
+            wk_raw[a, n0] = raw
+
+        def split_wk(a, n0, n1):
+            w = n1 - n0
+            raw = wk_raw[a, n0]
+            parts = keep.tile([P, 2, w, PACK], BF16, name=f"wk_parts_{a}_{n0}", align_bytes=64)
+            hi = parts[:, 0, :, :].rearrange("p (c e) i -> p c i e", e=2)
+            lo = parts[:, 1, :, :].rearrange("p (c e) i -> p c i e", e=2)
+            upper = raw[:].bitcast(BF16).rearrange("p i (c e h) -> p c i e h", e=2, h=2)[:, :, :, :, 1]
+            nc.scalar.copy(hi, upper)
+            pairs = parts[:, 0, :, :].rearrange("p n i -> p (n i)").bitcast(I32)
+            nc.vector.tensor_scalar(pairs, pairs, HI_MASK, None, ALU.bitwise_and)
+            nc.vector.tensor_tensor(lo, raw[:].rearrange("p i (c e) -> p c i e", e=2), hi, ALU.subtract)
+            codes = keep.tile([P, 2, w], U32, name=f"wk_codes_{a}_{n0}", align_bytes=64)
+            scales = keep.tile([P, 2, w], U8, name=f"wk_scales_{a}_{n0}", align_bytes=64)
+            nc.vector.quantize_mx(
+                out=codes[:].rearrange("p h n -> p (h n)").bitcast(FP8X4),
+                scales=scales[:].rearrange("p h n -> p (h n)"),
+                in_=parts[:].rearrange("p h n i -> p (h n i)"),
+            )
+            for nt in range(n0 // P, n1 // P):
+                cols = slice(nt * P - n0, (nt + 1) * P - n0)
+                wk_q[a, nt] = [(codes[:, h, cols], scales[:, h, cols]) for h in range(2)]
+
+        early = [(0, 0, 128), (0, 128, 256), (1, 0, 256)]
+        late = [(0, 256, 512), (1, 256, 512)]
+
+        nc.sync.dma_start(offs_t[:], offs)
+        for piece in early:
+            load_wk(*piece)
+        nc.sync.dma_start(wgt_t[:], wgt)
+        planes = {}
+        for a in range(PASSES):
+            for i in range(PACK):
+                pl = ring.tile([P, T], F32, name=f"plane_{a}_{i}", tag="plane", bufs=PASSES * PACK)
+                nc.sync.dma_start(pl[:], x_rows[a, i])
+                planes[a, i] = pl
+            if a == 0:
+                for q in range(4):
+                    nc.sync.dma_start(
+                        wv_sc[32 * q : 32 * q + 4, :, :].bitcast(I32),
+                        wv_scales[:, 4 * q : 4 * q + 4, :].rearrange("a r n -> r a n").bitcast(I32),
+                    )
+                with nc.allow_non_contiguous_dma(reason="one bias value a partition"):
+                    nc.sync.dma_start(bg_t[:], bg.rearrange("(c p) -> p c", p=P))
+                nc.sync.dma_start(offs2_t[:], offs2)
+        nc.sync.dma_start(wv_codes[:].bitcast(I32), wv_words.rearrange("a p n i -> p a (n i)").bitcast(I32))
+        res_t = {}
+
+        def load_res(nt, jh):
+            r = ring.tile([P, JH], F32, name=f"res_{nt}_{jh}", tag="res", bufs=4)
+            nc.sync.dma_start(r[:], res[nt * P : (nt + 1) * P, jh * JH : (jh + 1) * JH])
+            res_t[nt, jh] = r
+
+        load_res(0, 0)
+        load_wk(*late[0])
+        load_wk(*late[1])
+        nc.sync.dma_start(wgo_t[:], wgo)
+        for jh in range(HALVES):
+            for nt in range(NT):
+                if (nt, jh) != (0, 0):
+                    load_res(nt, jh)
+
+        for piece in early:
+            split_wk(*piece)
+
+        xq = {}
+
+        def gather(a, jh):
+            picked = ring.tile([P, PACK, JH], F32, name=f"picked_{a}_{jh}", tag="picked", bufs=3)
+            lst = offs_t[:, jh * LIST_COLS : (jh + 1) * LIST_COLS]
+            for i in range(PACK):
+                nc.vector.tensor_tensor(
+                    picked[:, i, :], planes[a, i][:].indirect(lst), wgt_t[:, jh * JH : (jh + 1) * JH], ALU.mult
+                )
+            grouped = ring.tile([P, JH, PACK], BF16, name=f"grouped_{a}_{jh}", tag="grouped", bufs=2, align_bytes=64)
+            nc.scalar.copy(
+                grouped[:].rearrange("p (c e) i -> p c i e", e=2),
+                picked[:].rearrange("p i (c e) -> p c i e", e=2),
+            )
+            codes = keep.tile([P, JH], U32, name=f"x_codes_{a}_{jh}", align_bytes=64)
+            scales = keep.tile([P, JH], U8, name=f"x_scales_{a}_{jh}", align_bytes=64)
+            nc.vector.quantize_mx(
+                out=codes[:].bitcast(FP8X4), scales=scales[:], in_=grouped[:].rearrange("p j i -> p (j i)")
+            )
+            xq[a, jh] = (codes, scales)
+
+        gather(0, 0)
+        gather(1, 0)
+
+        def late_weights():
+            for piece in late:
+                split_wk(*piece)
+
+        def second_half():
+            gather(0, 1)
+            gather(1, 1)
+            for nt in range(2, NT):
+                w = ring.tile([P, T], F32, name=f"win{nt}", tag="plane", bufs=PASSES * PACK)
+                for c in range(0, T, JH):
+                    nc.gpsimd.memset(w[:, c : c + JH], 0.0)
+                windows.append(w)
+
+        tiles = [(nt, jh) for jh in range(HALVES) for nt in range(NT)]
+        gate, veT, diff, neg_resT, neg_mixT, full = {}, {}, {}, {}, {}, {}
+        JB = JH // P
+
+        def transpose_blocks(bank, sources):
+            for jb in range(JB):
+                cols = slice(jb * P, (jb + 1) * P)
+                for s, src in enumerate(sources):
+                    nc.tensor.matmul(
+                        bank[:, cols], src[:, cols], ident[:], is_transpose=True,
+                        start=(s == 0), stop=(s == len(sources) - 1),
+                    )
+
+        def turn_res(nt, jh):
+            bank = psum.tile([P, JH], F32, name=f"resT_ps_{nt}_{jh}", tag="resT", bufs=1)
+            transpose_blocks(bank, [res_t[nt, jh]])
+            r = ring.tile([P, JH], F32, name=f"neg_resT_{nt}_{jh}", tag="neg_resT", bufs=8)
+            nc.scalar.activation(r[:], bank[:], ACT.Copy, scale=-1.0)
+            neg_resT[nt, jh] = r
+
+        def products(nt, jh):
+            cols = slice(nt * P, (nt + 1) * P)
+            ve = psum.tile([P, JH], F32, name=f"veT_ps_{nt}_{jh}", tag="veT", bufs=1)
+            for jb in range(JB):
+                jcols = slice(jb * P, (jb + 1) * P)
+                for a in range(PASSES):
+                    xc, xs = xq[a, jh]
+                    nc.tensor.matmul_mx(
+                        out=ve[:, jcols], lhsT=xc[:, jcols].bitcast(FP8X4), lhsT_scale=xs[:, jcols],
+                        rhs=wv_codes[:, a, cols].bitcast(FP8X4), rhs_scale=wv_sc[:, a, cols],
+                        start=(a == 0), stop=(a == PASSES - 1),
+                    )
+            v = ring.tile([P, JH], F32, name=f"veT_{nt}_{jh}", tag="veT_sb", bufs=4)
+            nc.scalar.copy(v[:], ve[:])
+            veT[nt, jh] = v
+            ke = psum.tile([P, JH], F32, name=f"ke_{nt}_{jh}", tag="ke", bufs=2)
+            steps = [(a, h) for a in range(PASSES) for h in range(2)]
+            for s, (a, h) in enumerate(steps):
+                wc, ws = wk_q[a, nt][h]
+                xc, xs = xq[a, jh]
+                nc.tensor.matmul_mx(
+                    out=ke[:], lhsT=wc.bitcast(FP8X4), lhsT_scale=ws, rhs=xc[:].bitcast(FP8X4), rhs_scale=xs[:],
+                    start=(s == 0), stop=(s == len(steps) - 1),
+                )
+            g = ring.tile([P, JH], F32, name=f"gate_{nt}_{jh}", tag="gate", bufs=4)
+            nc.scalar.activation(g[:], ke[:], ACT.Sigmoid, bias=bg_t[:, nt : nt + 1])
+            gate[nt, jh] = g
+
+        def difference(nt, jh):
+            bank = psum.tile([P, JH], F32, name=f"diff_ps_{nt}_{jh}", tag="diff", bufs=2)
+            transpose_blocks(bank, [veT[nt, jh], neg_resT[nt, jh]])
+            diff[nt, jh] = bank
+
+        def mix(nt, jh):
+            m = ring.tile([P, JH], F32, name=f"mixed_{nt}_{jh}", tag="mixed", bufs=2)
+            nc.vector.tensor_tensor(m[:], diff[nt, jh][:], gate[nt, jh][:], ALU.mult)
+            bank = psum.tile([P, JH], F32, name=f"mixT_ps_{nt}_{jh}", tag="mixT", bufs=1)
+            transpose_blocks(bank, [m])
+            mt = ring.tile([P, JH], F32, name=f"neg_mixT_{nt}_{jh}", tag="neg_mixT", bufs=2)
+            nc.scalar.activation(mt[:], bank[:], ACT.Copy, scale=-1.0)
+            neg_mixT[nt, jh] = mt
+
+        def add_res(nt, jh):
+            bank = psum.tile([P, JH], F32, name=f"full_ps_{nt}_{jh}", tag="full", bufs=1)
+            transpose_blocks(bank, [neg_mixT[nt, jh], neg_resT[nt, jh]])
+            f = ring.tile([P, JH], F32, name=f"full_{nt}_{jh}", tag="full_sb", bufs=3)
+            nc.scalar.activation(f[:], bank[:], ACT.Copy, scale=-1.0)
+            full[nt, jh] = f
+
+        def scatter(nt, jh):
+            lst = offs2_t[:, jh * LIST_COLS : (jh + 1) * LIST_COLS]
+            nc.vector.tensor_tensor(
+                windows[nt][:].indirect(lst), full[nt, jh][:], wgo_t[:, jh * JH : (jh + 1) * JH], ALU.mult
+            )
+            if jh == HALVES - 1:
+                nc.sync.dma_start(out[nt * P : (nt + 1) * P, :], windows[nt][:])
+
+        stages = [(add_res, 3), (mix, 2), (difference, 1), (scatter, 4), (turn_res, 0), (products, 0)]
+        for step in range(len(tiles) + 4):
+            for stage, lag in stages:
+                if stage is products and step == 2:
+                    late_weights()
+                if stage is products and step == 3:
+                    second_half()
+                if 0 <= step - lag < len(tiles):
+                    stage(*tiles[step - lag])

@@ -23,6 +23,7 @@ JH = 512
 HALVES = J // JH
 NT = N // P
 LIST_COLS = JH // 16
+EARLY = 768
 HI_MASK = 0xFFF0FFF0 - (1 << 32)
 
 
@@ -33,11 +34,13 @@ def tile_list_hl_hwayS_kernel(
     with ExitStack() as ctx:
         keep = ctx.enter_context(tc.tile_pool(name="keep", bufs=1))
         ring = ctx.enter_context(tc.tile_pool(name="ring", bufs=1))
+        shared = ctx.enter_context(tc.tile_pool(name="shared", bufs=1))
         psum = ctx.enter_context(tc.psum_pool(name="psum", bufs=1))
 
         offs_t = keep.tile([P, J // 16], U16, name="offs_t")
         offs2_t = keep.tile([P, J // 16], U16, name="offs2_t")
-        wgt_t = keep.tile([P, J], F32, name="wgt_t")
+        wgt_head = shared.tile([P, EARLY], F32, name="wgt_head", offset=1024)
+        wgt_tail = keep.tile([P, JH], F32, name="wgt_tail")
         wgo_t = keep.tile([P, J], F32, name="wgo_t")
         bg_t = keep.tile([P, NT], F32, name="bg_t")
         wv_codes = keep.tile([P, PASSES, N], U32, name="wv_codes", align_bytes=64)
@@ -58,22 +61,24 @@ def tile_list_hl_hwayS_kernel(
         wk_raw = {}
         wk_q = {}
 
-        def load_wk(a, n0, n1):
-            raw = keep.tile([P, PACK, n1 - n0], F32, name=f"wk_raw_{a}_{n0}")
-            nc.sync.dma_start(raw[:], wk_rows[a][:, :, n0:n1])
-            wk_raw[a, n0] = raw
+        def load_wk(a):
+            raw = keep.tile([P, PACK, N], F32, name=f"wk_raw_{a}")
+            nc.sync.dma_start(raw[:], wk_rows[a])
+            wk_raw[a] = raw
 
         def split_wk(a, n0, n1):
             w = n1 - n0
-            raw = wk_raw[a, n0]
-            parts = keep.tile([P, 2, w, PACK], BF16, name=f"wk_parts_{a}_{n0}", align_bytes=64)
+            raw = wk_raw[a][:, :, n0:n1]
+            parts = ring.tile(
+                [P, 2, w, PACK], BF16, name=f"wk_parts_{a}_{n0}", tag="wk_parts", bufs=3, align_bytes=64
+            )
             hi = parts[:, 0, :, :].rearrange("p (c e) i -> p c i e", e=2)
             lo = parts[:, 1, :, :].rearrange("p (c e) i -> p c i e", e=2)
-            upper = raw[:].bitcast(BF16).rearrange("p i (c e h) -> p c i e h", e=2, h=2)[:, :, :, :, 1]
+            upper = raw.bitcast(BF16).rearrange("p i (c e h) -> p c i e h", e=2, h=2)[:, :, :, :, 1]
             nc.scalar.copy(hi, upper)
             pairs = parts[:, 0, :, :].rearrange("p n i -> p (n i)").bitcast(I32)
             nc.vector.tensor_scalar(pairs, pairs, HI_MASK, None, ALU.bitwise_and)
-            nc.vector.tensor_tensor(lo, raw[:].rearrange("p i (c e) -> p c i e", e=2), hi, ALU.subtract)
+            nc.vector.tensor_tensor(lo, raw.rearrange("p i (c e) -> p c i e", e=2), hi, ALU.subtract)
             codes = keep.tile([P, 2, w], U32, name=f"wk_codes_{a}_{n0}", align_bytes=64)
             scales = keep.tile([P, 2, w], U8, name=f"wk_scales_{a}_{n0}", align_bytes=64)
             nc.vector.quantize_mx(
@@ -85,62 +90,65 @@ def tile_list_hl_hwayS_kernel(
                 cols = slice(nt * P - n0, (nt + 1) * P - n0)
                 wk_q[a, nt] = [(codes[:, h, cols], scales[:, h, cols]) for h in range(2)]
 
-        early = [(0, 0, 128), (0, 128, 256), (1, 0, 256)]
-        late = [(0, 256, 512), (1, 256, 512)]
-
-        nc.sync.dma_start(offs_t[:], offs)
-        for piece in early:
-            load_wk(*piece)
-        nc.sync.dma_start(wgt_t[:], wgt)
         planes = {}
-        for a in range(PASSES):
-            for i in range(PACK):
-                pl = ring.tile([P, T], F32, name=f"plane_{a}_{i}", tag="plane", bufs=PASSES * PACK)
-                nc.sync.dma_start(pl[:], x_rows[a, i])
-                planes[a, i] = pl
-            if a == 0:
-                for q in range(4):
-                    nc.sync.dma_start(
-                        wv_sc[32 * q : 32 * q + 4, :, :].bitcast(I32),
-                        wv_scales[:, 4 * q : 4 * q + 4, :].rearrange("a r n -> r a n").bitcast(I32),
-                    )
-                with nc.allow_non_contiguous_dma(reason="one bias value a partition"):
-                    nc.sync.dma_start(bg_t[:], bg.rearrange("(c p) -> p c", p=P))
-                nc.sync.dma_start(offs2_t[:], offs2)
-        nc.sync.dma_start(wv_codes[:].bitcast(I32), wv_words.rearrange("a p n i -> p a (n i)").bitcast(I32))
         res_t = {}
 
+        def load_planes(a):
+            for i in range(PACK):
+                pl = ring.tile([P, T], F32, name=f"plane_{a}_{i}", tag=f"plane{a}", bufs=PACK)
+                nc.sync.dma_start(pl[:], x_rows[a, i])
+                planes[a, i] = pl
+
         def load_res(nt, jh):
-            r = ring.tile([P, JH], F32, name=f"res_{nt}_{jh}", tag="res", bufs=4)
+            r = ring.tile([P, JH], F32, name=f"res_{nt}_{jh}", tag="res", bufs=8)
             nc.sync.dma_start(r[:], res[nt * P : (nt + 1) * P, jh * JH : (jh + 1) * JH])
             res_t[nt, jh] = r
 
-        load_res(0, 0)
-        load_wk(*late[0])
-        load_wk(*late[1])
+        load_wk(0)
+        nc.sync.dma_start(offs_t[:], offs)
+        nc.sync.dma_start(wgt_head[:], wgt[:, :EARLY])
+        load_planes(0)
+        load_wk(1)
+        for q in range(4):
+            nc.sync.dma_start(
+                wv_sc[32 * q : 32 * q + 4, :, :].bitcast(I32),
+                wv_scales[:, 4 * q : 4 * q + 4, :].rearrange("a r n -> r a n").bitcast(I32),
+            )
+        with nc.allow_non_contiguous_dma(reason="one bias value a partition"):
+            nc.sync.dma_start(bg_t[:], bg.rearrange("(c p) -> p c", p=P))
+        nc.sync.dma_start(offs2_t[:], offs2)
+        load_planes(1)
+        nc.sync.dma_start(wgt_tail[:], wgt[:, JH:])
+        nc.sync.dma_start(wv_codes[:].bitcast(I32), wv_words.rearrange("a p n i -> p a (n i)").bitcast(I32))
+        for nt in range(NT):
+            load_res(nt, 0)
         nc.sync.dma_start(wgo_t[:], wgo)
-        for jh in range(HALVES):
-            for nt in range(NT):
-                if (nt, jh) != (0, 0):
-                    load_res(nt, jh)
-
-        for piece in early:
-            split_wk(*piece)
+        for nt in range(NT):
+            load_res(nt, 1)
 
         xq = {}
 
-        def gather(a, jh):
-            picked = ring.tile([P, PACK, JH], F32, name=f"picked_{a}_{jh}", tag="picked", bufs=3)
-            lst = offs_t[:, jh * LIST_COLS : (jh + 1) * LIST_COLS]
+        def gather(picked, a, j0, j1, weights):
             for i in range(PACK):
                 nc.vector.tensor_tensor(
-                    picked[:, i, :], planes[a, i][:].indirect(lst), wgt_t[:, jh * JH : (jh + 1) * JH], ALU.mult
+                    picked[:, i, :], planes[a, i][:].indirect(offs_t[:, j0 // 16 : j1 // 16]), weights, ALU.mult
                 )
-            grouped = ring.tile([P, JH, PACK], BF16, name=f"grouped_{a}_{jh}", tag="grouped", bufs=2, align_bytes=64)
-            nc.scalar.copy(
-                grouped[:].rearrange("p (c e) i -> p c i e", e=2),
-                picked[:].rearrange("p i (c e) -> p c i e", e=2),
-            )
+
+        def quantize_x(a, jh, sources):
+            if (a, jh) == (1, 1):
+                grouped = shared.tile([P, JH, PACK], BF16, name="grouped_last", offset=8192, align_bytes=64)
+            else:
+                grouped = ring.tile(
+                    [P, JH, PACK], BF16, name=f"grouped_{a}_{jh}", tag="grouped", bufs=2, align_bytes=64
+                )
+            j0 = 0
+            for src in sources:
+                j1 = j0 + src.shape[2]
+                nc.scalar.copy(
+                    grouped[:, j0:j1, :].rearrange("p (c e) i -> p c i e", e=2),
+                    src.rearrange("p i (c e) -> p c i e", e=2),
+                )
+                j0 = j1
             codes = keep.tile([P, JH], U32, name=f"x_codes_{a}_{jh}", align_bytes=64)
             scales = keep.tile([P, JH], U8, name=f"x_scales_{a}_{jh}", align_bytes=64)
             nc.vector.quantize_mx(
@@ -148,18 +156,26 @@ def tile_list_hl_hwayS_kernel(
             )
             xq[a, jh] = (codes, scales)
 
-        gather(0, 0)
-        gather(1, 0)
-
-        def late_weights():
-            for piece in late:
-                split_wk(*piece)
+        for n0, n1 in ((0, 128), (128, 256), (256, 512)):
+            split_wk(0, n0, n1)
+        picked_head = keep.tile([P, PACK, EARLY], F32, name="picked_head")
+        gather(picked_head, 0, 0, EARLY, wgt_head[:])
+        quantize_x(0, 0, [picked_head[:, :, :JH]])
+        for n0, n1 in ((0, 256), (256, 512)):
+            split_wk(1, n0, n1)
+        picked = ring.tile([P, PACK, JH], F32, name="picked_1_0", tag="picked", bufs=1)
+        gather(picked, 1, 0, JH, wgt_head[:, :JH])
+        quantize_x(1, 0, [picked[:]])
 
         def second_half():
-            gather(0, 1)
-            gather(1, 1)
+            picked_tail = shared.tile([P, PACK, J - EARLY], F32, name="picked_tail", offset=2048)
+            gather(picked_tail, 0, EARLY, J, wgt_tail[:, EARLY - JH :])
+            quantize_x(0, 1, [picked_head[:, :, JH:], picked_tail[:]])
+            picked_last = ring.tile([P, PACK, JH], F32, name="picked_1_1", tag="picked", bufs=1)
+            gather(picked_last, 1, JH, J, wgt_tail[:])
+            quantize_x(1, 1, [picked_last[:]])
             for nt in range(2, NT):
-                w = ring.tile([P, T], F32, name=f"win{nt}", tag="plane", bufs=PASSES * PACK)
+                w = ring.tile([P, T], F32, name=f"win{nt}", tag="plane1", bufs=PACK)
                 for c in range(0, T, JH):
                     nc.gpsimd.memset(w[:, c : c + JH], 0.0)
                 windows.append(w)
@@ -167,6 +183,8 @@ def tile_list_hl_hwayS_kernel(
         tiles = [(nt, jh) for jh in range(HALVES) for nt in range(NT)]
         gate, veT, diff, neg_resT, neg_mixT, full = {}, {}, {}, {}, {}, {}
         JB = JH // P
+        mixed = {}
+        on_tensor = tiles[1:7]
 
         def transpose_blocks(bank, sources):
             for jb in range(JB):
@@ -180,7 +198,10 @@ def tile_list_hl_hwayS_kernel(
         def turn_res(nt, jh):
             bank = psum.tile([P, JH], F32, name=f"resT_ps_{nt}_{jh}", tag="resT", bufs=1)
             transpose_blocks(bank, [res_t[nt, jh]])
-            r = ring.tile([P, JH], F32, name=f"neg_resT_{nt}_{jh}", tag="neg_resT", bufs=8)
+            if (nt, jh) == tiles[0]:
+                r = shared.tile([P, JH], F32, name="neg_resT_first", offset=0)
+            else:
+                r = ring.tile([P, JH], F32, name=f"neg_resT_{nt}_{jh}", tag="neg_resT", bufs=3)
             nc.scalar.activation(r[:], bank[:], ACT.Copy, scale=-1.0)
             neg_resT[nt, jh] = r
 
@@ -196,7 +217,10 @@ def tile_list_hl_hwayS_kernel(
                         rhs=wv_codes[:, a, cols].bitcast(FP8X4), rhs_scale=wv_sc[:, a, cols],
                         start=(a == 0), stop=(a == PASSES - 1),
                     )
-            v = ring.tile([P, JH], F32, name=f"veT_{nt}_{jh}", tag="veT_sb", bufs=4)
+            if (nt, jh) == tiles[1]:
+                v = shared.tile([P, JH], F32, name="veT_second", offset=8192)
+            else:
+                v = ring.tile([P, JH], F32, name=f"veT_{nt}_{jh}", tag="veT_sb", bufs=3)
             nc.scalar.copy(v[:], ve[:])
             veT[nt, jh] = v
             ke = psum.tile([P, JH], F32, name=f"ke_{nt}_{jh}", tag="ke", bufs=2)
@@ -208,7 +232,10 @@ def tile_list_hl_hwayS_kernel(
                     out=ke[:], lhsT=wc.bitcast(FP8X4), lhsT_scale=ws, rhs=xc[:].bitcast(FP8X4), rhs_scale=xs[:],
                     start=(s == 0), stop=(s == len(steps) - 1),
                 )
-            g = ring.tile([P, JH], F32, name=f"gate_{nt}_{jh}", tag="gate", bufs=4)
+            if (nt, jh) == tiles[1]:
+                g = shared.tile([P, JH], F32, name="gate_second", offset=12288)
+            else:
+                g = ring.tile([P, JH], F32, name=f"gate_{nt}_{jh}", tag="gate", bufs=3)
             nc.scalar.activation(g[:], ke[:], ACT.Sigmoid, bias=bg_t[:, nt : nt + 1])
             gate[nt, jh] = g
 
@@ -220,6 +247,9 @@ def tile_list_hl_hwayS_kernel(
         def mix(nt, jh):
             m = ring.tile([P, JH], F32, name=f"mixed_{nt}_{jh}", tag="mixed", bufs=2)
             nc.vector.tensor_tensor(m[:], diff[nt, jh][:], gate[nt, jh][:], ALU.mult)
+            mixed[nt, jh] = m
+            if (nt, jh) not in on_tensor:
+                return
             bank = psum.tile([P, JH], F32, name=f"mixT_ps_{nt}_{jh}", tag="mixT", bufs=1)
             transpose_blocks(bank, [m])
             mt = ring.tile([P, JH], F32, name=f"neg_mixT_{nt}_{jh}", tag="neg_mixT", bufs=2)
@@ -227,6 +257,14 @@ def tile_list_hl_hwayS_kernel(
             neg_mixT[nt, jh] = mt
 
         def add_res(nt, jh):
+            if (nt, jh) not in on_tensor:
+                if (nt, jh) == tiles[0]:
+                    f = shared.tile([P, JH], F32, name="full_first", offset=12288)
+                else:
+                    f = ring.tile([P, JH], F32, name=f"full_{nt}_{jh}", tag="full_sb", bufs=3)
+                nc.vector.tensor_tensor(f[:], mixed[nt, jh][:], res_t[nt, jh][:], ALU.add)
+                full[nt, jh] = f
+                return
             bank = psum.tile([P, JH], F32, name=f"full_ps_{nt}_{jh}", tag="full", bufs=1)
             transpose_blocks(bank, [neg_mixT[nt, jh], neg_resT[nt, jh]])
             f = ring.tile([P, JH], F32, name=f"full_{nt}_{jh}", tag="full_sb", bufs=3)
@@ -241,12 +279,14 @@ def tile_list_hl_hwayS_kernel(
             if jh == HALVES - 1:
                 nc.sync.dma_start(out[nt * P : (nt + 1) * P, :], windows[nt][:])
 
-        stages = [(add_res, 3), (mix, 2), (difference, 1), (scatter, 4), (turn_res, 0), (products, 0)]
-        for step in range(len(tiles) + 4):
+        stages = [(mix, 0), (difference, -1), (add_res, 0), (scatter, 1), (turn_res, -2), (products, -2)]
+        for step in range(-2, len(tiles) + 1):
             for stage, lag in stages:
-                if stage is products and step == 2:
-                    late_weights()
-                if stage is products and step == 3:
+                if stage is products and step == 1:
                     second_half()
+                if stage is add_res and step == 0:
+                    continue
+                if stage is add_res and step == 1:
+                    add_res(*tiles[0])
                 if 0 <= step - lag < len(tiles):
                     stage(*tiles[step - lag])

@@ -19,12 +19,27 @@ ACT = mybir.ActivationFunctionType
 P = 128
 PACK = 4
 PASSES = K // (P * PACK)
+GROUP = 16
 JH = 512
 HALVES = J // JH
 NT = N // P
-LIST_COLS = JH // 16
-EARLY = 768
-HI_MASK = 0xFFF0FFF0 - (1 << 32)
+BLOCKS = JH // P
+TILE_BYTES = JH * 4
+PLANE_BYTES = T * 4
+
+HI_MASK = 0xFFF00000 - (1 << 32)
+PAIR_MASK = 0xFFF0FFF0 - (1 << 32)
+SIGN_BIT = -(1 << 31)
+
+WK_COLS = 256
+HEAD0 = 896
+HEAD1 = 640
+WIDE_PLANES = 2
+SUM_ON_VECTOR = (0, 1, 3)
+AHEAD = 2
+TURN_SLOTS = 4
+GATE_SLOTS = 3
+MIX_SLOTS = 4
 
 
 def tile_list_hl_hwayS_kernel(
@@ -35,11 +50,12 @@ def tile_list_hl_hwayS_kernel(
         keep = ctx.enter_context(tc.tile_pool(name="keep", bufs=1))
         ring = ctx.enter_context(tc.tile_pool(name="ring", bufs=1))
         shared = ctx.enter_context(tc.tile_pool(name="shared", bufs=1))
+        reuse = ctx.enter_context(tc.tile_pool(name="reuse", bufs=1))
         psum = ctx.enter_context(tc.psum_pool(name="psum", bufs=1))
 
-        offs_t = keep.tile([P, J // 16], U16, name="offs_t")
-        offs2_t = keep.tile([P, J // 16], U16, name="offs2_t")
-        wgt_head = shared.tile([P, EARLY], F32, name="wgt_head", offset=1024)
+        offs_t = keep.tile([P, J // GROUP], U16, name="offs_t")
+        offs2_t = keep.tile([P, J // GROUP], U16, name="offs2_t")
+        wgt_head = shared.tile([P, HEAD0], F32, name="wgt_head", offset=1024)
         wgt_tail = keep.tile([P, JH], F32, name="wgt_tail")
         wgo_t = keep.tile([P, J], F32, name="wgo_t")
         bg_t = keep.tile([P, NT], F32, name="bg_t")
@@ -48,245 +64,303 @@ def tile_list_hl_hwayS_kernel(
 
         x_rows = xT.rearrange("(a p i) t -> a i p t", a=PASSES, i=PACK)
         wk_rows = wk.rearrange("(a p i) n -> a p i n", a=PASSES, i=PACK)
+        res_rows = res.rearrange("(c p) j -> p c j", p=P)
 
         ident = keep.tile([P, P], F32, name="ident")
         make_identity(nc, ident[:])
         nc.vector.memset(wv_sc[:].bitcast(I32), 0)
         windows = []
-        for nt in range(2):
-            w = keep.tile([P, T], F32, name=f"win{nt}")
-            nc.vector.memset(w[:], 0.0)
-            windows.append(w)
+        for nt in range(NT // 2):
+            window = keep.tile([P, T], F32, name=f"win{nt}")
+            nc.vector.memset(window[:].bitcast(I32), 0)
+            windows.append(window)
 
-        wk_raw = {}
-        wk_q = {}
+        wk_raw, planes, res_half = {}, {}, {}
+        wk_q, xq = {}, {}
 
         def load_wk(a):
-            raw = keep.tile([P, PACK, N], F32, name=f"wk_raw_{a}")
-            nc.sync.dma_start(raw[:], wk_rows[a])
-            wk_raw[a] = raw
+            wk_raw[a] = ring.tile([P, PACK, N], F32, name=f"wk_raw_{a}", tag="wk_raw", bufs=PASSES)
+            nc.sync.dma_start(wk_raw[a][:], wk_rows[a])
 
-        def split_wk(a, n0, n1):
-            w = n1 - n0
-            raw = wk_raw[a][:, :, n0:n1]
-            parts = ring.tile(
-                [P, 2, w, PACK], BF16, name=f"wk_parts_{a}_{n0}", tag="wk_parts", bufs=3, align_bytes=64
-            )
-            hi = parts[:, 0, :, :].rearrange("p (c e) i -> p c i e", e=2)
-            lo = parts[:, 1, :, :].rearrange("p (c e) i -> p c i e", e=2)
-            upper = raw.bitcast(BF16).rearrange("p i (c e h) -> p c i e h", e=2, h=2)[:, :, :, :, 1]
-            nc.scalar.copy(hi, upper)
-            pairs = parts[:, 0, :, :].rearrange("p n i -> p (n i)").bitcast(I32)
-            nc.vector.tensor_scalar(pairs, pairs, HI_MASK, None, ALU.bitwise_and)
-            nc.vector.tensor_tensor(lo, raw.rearrange("p i (c e) -> p c i e", e=2), hi, ALU.subtract)
-            codes = keep.tile([P, 2, w], U32, name=f"wk_codes_{a}_{n0}", align_bytes=64)
-            scales = keep.tile([P, 2, w], U8, name=f"wk_scales_{a}_{n0}", align_bytes=64)
+        def load_plane(a, i):
+            if a == 0:
+                plane = reuse.tile([P, T], F32, name=f"plane_{a}_{i}", offset=i * PLANE_BYTES)
+            else:
+                plane = ring.tile([P, T], F32, name=f"plane_{a}_{i}", tag="plane1", bufs=PACK)
+            nc.sync.dma_start(plane[:], x_rows[a, i])
+            planes[a, i] = plane
+
+        def load_res(jh, nt0, nt1):
+            if nt0 == 0:
+                res_half[jh] = ring.tile([P, NT, JH], F32, name=f"res_{jh}", tag="wk_raw", bufs=PASSES)
+            nc.sync.dma_start(res_half[jh][:, nt0:nt1, :], res_rows[:, nt0:nt1, jh * JH : (jh + 1) * JH])
+
+        def transpose_sum(bank, sources):
+            for b in range(BLOCKS):
+                for s, source in enumerate(sources):
+                    nc.tensor.matmul(
+                        bank[:, b * P : (b + 1) * P], source(b), ident[:], is_transpose=True,
+                        start=(s == 0), stop=(s == len(sources) - 1),
+                    )
+
+        def blocks(t):
+            return lambda b: t[:, b * P : (b + 1) * P]
+
+        def by_plane(ap):
+            return ap.rearrange("p i (c e) -> p c i e", e=2)
+
+        def by_column(ap):
+            return ap.rearrange("p (c e) i -> p c i e", e=2)
+
+        def quantize_wk(a, n0, part):
+            width = part[:].shape[2]
+            codes = keep.tile([P, 2, width], U32, name=f"wk_codes_{a}_{n0}", align_bytes=64)
+            scales = keep.tile([P, 2, width], U8, name=f"wk_scales_{a}_{n0}", align_bytes=64)
             nc.vector.quantize_mx(
                 out=codes[:].rearrange("p h n -> p (h n)").bitcast(FP8X4),
                 scales=scales[:].rearrange("p h n -> p (h n)"),
-                in_=parts[:].rearrange("p h n i -> p (h n i)"),
+                in_=part[:].rearrange("p h n i -> p (h n i)"),
             )
-            for nt in range(n0 // P, n1 // P):
-                cols = slice(nt * P - n0, (nt + 1) * P - n0)
-                wk_q[a, nt] = [(codes[:, h, cols], scales[:, h, cols]) for h in range(2)]
+            for c in range(0, width, P):
+                wk_q[a, (n0 + c) // P] = [(codes[:, h, c : c + P], scales[:, h, c : c + P]) for h in range(2)]
 
-        planes = {}
-        res_t = {}
+        def split_on_tensor(a, n0):
+            raw = wk_raw[a]
+            neg_hi = ring.tile([P, PACK, WK_COLS], F32, name=f"neg_hi_{a}_{n0}", tag="neg_hi", bufs=2)
+            part = ring.tile(
+                [P, 2, WK_COLS, PACK], BF16, name=f"wk_parts_{a}_{n0}", tag="wk_parts", bufs=2, align_bytes=64
+            )
+            nc.vector.tensor_scalar(
+                neg_hi[:].bitcast(I32), raw[:, :, n0 : n0 + WK_COLS].bitcast(I32),
+                HI_MASK, SIGN_BIT, ALU.bitwise_and, ALU.bitwise_xor,
+            )
+            for c in range(0, WK_COLS, P):
+                turned = psum.tile([P, JH], F32, name=f"loT_ps_{a}_{n0 + c}", tag="diff", bufs=2)
+                transpose_sum(turned, [lambda i: raw[:, i, n0 + c : n0 + c + P], lambda i: neg_hi[:, i, c : c + P]])
+                lo_t = ring.tile([P, JH], F32, name=f"loT_{a}_{n0 + c}", tag="spare", bufs=2)
+                nc.scalar.copy(lo_t[:], turned[:])
+                back = psum.tile([P, JH], F32, name=f"lo_ps_{a}_{n0 + c}", tag="full")
+                transpose_sum(back, [blocks(lo_t)])
+                nc.scalar.copy(part[:, 1, c : c + P, :], back[:].rearrange("p (i n) -> p n i", i=PACK))
+            nc.scalar.activation(by_column(part[:, 0, :, :]), by_plane(neg_hi[:]), ACT.Copy, scale=-1.0)
+            quantize_wk(a, n0, part)
 
-        def load_planes(a):
-            for i in range(PACK):
-                pl = ring.tile([P, T], F32, name=f"plane_{a}_{i}", tag=f"plane{a}", bufs=PACK)
-                nc.sync.dma_start(pl[:], x_rows[a, i])
-                planes[a, i] = pl
+        def split_on_vector(a, n0):
+            starts = range(n0, n0 + WK_COLS, P)
+            raws = [wk_raw[a][:, :, c : c + P] for c in starts]
+            parts = []
+            for c, raw in zip(starts, raws):
+                part = ring.tile(
+                    [P, 2, P, PACK], BF16, name=f"wk_parts_{a}_{c}", tag="wk_parts_v", bufs=2, align_bytes=64
+                )
+                halves = raw.bitcast(BF16).rearrange("p i (c e h) -> p c i e h", e=2, h=2)
+                nc.scalar.copy(by_column(part[:, 0, :, :]), halves[:, :, :, :, 1])
+                parts.append(part)
 
-        def load_res(nt, jh):
-            r = ring.tile([P, JH], F32, name=f"res_{nt}_{jh}", tag="res", bufs=8)
-            nc.sync.dma_start(r[:], res[nt * P : (nt + 1) * P, jh * JH : (jh + 1) * JH])
-            res_t[nt, jh] = r
+            def mask(part):
+                pairs = part[:, 0, :, :].rearrange("p n i -> p (n i)").bitcast(I32)
+                nc.vector.tensor_scalar(pairs, pairs, PAIR_MASK, None, ALU.bitwise_and)
+
+            mask(parts[0])
+            for u, part in enumerate(parts):
+                nc.vector.tensor_tensor(
+                    by_column(part[:, 1, :, :]), by_plane(raws[u]), by_column(part[:, 0, :, :]), ALU.subtract
+                )
+                if u + 1 < len(parts):
+                    mask(parts[u + 1])
+                quantize_wk(a, starts[u], part)
+
+        def gather(dst, a, i, j0, j1):
+            weights = wgt_head[:, j0:j1] if j0 == 0 else wgt_tail[:, j0 - JH : j1 - JH]
+            nc.vector.tensor_tensor(
+                dst, planes[a, i][:].indirect(offs_t[:, j0 // GROUP : j1 // GROUP]), weights, ALU.mult
+            )
+
+        def interleave(grouped, picked):
+            nc.scalar.copy(by_column(grouped), by_plane(picked))
+
+        def quantize_x(a, jh, grouped):
+            codes = keep.tile([P, JH], U32, name=f"x_codes_{a}_{jh}", align_bytes=64)
+            scales = keep.tile([P, JH], U8, name=f"x_scales_{a}_{jh}", align_bytes=64)
+            nc.vector.quantize_mx(
+                out=codes[:].bitcast(FP8X4), scales=scales[:], in_=grouped.rearrange("p j i -> p (j i)")
+            )
+            xq[a, jh] = (codes, scales)
 
         load_wk(0)
         nc.sync.dma_start(offs_t[:], offs)
-        nc.sync.dma_start(wgt_head[:], wgt[:, :EARLY])
-        load_planes(0)
         load_wk(1)
+        nc.sync.dma_start(wgt_head[:], wgt[:, :HEAD0])
+        plane_order = [(a, i) for a in range(PASSES) for i in range(PACK)]
+        for a, i in plane_order[:-1]:
+            load_plane(a, i)
         for q in range(4):
             nc.sync.dma_start(
                 wv_sc[32 * q : 32 * q + 4, :, :].bitcast(I32),
                 wv_scales[:, 4 * q : 4 * q + 4, :].rearrange("a r n -> r a n").bitcast(I32),
             )
-        with nc.allow_non_contiguous_dma(reason="one bias value a partition"):
-            nc.sync.dma_start(bg_t[:], bg.rearrange("(c p) -> p c", p=P))
-        nc.sync.dma_start(offs2_t[:], offs2)
-        load_planes(1)
+        load_plane(*plane_order[-1])
+
+        picked0 = keep.tile([P, PACK, HEAD0], F32, name="picked0")
+        grouped0 = keep.tile([P, J, PACK], BF16, name="grouped0", align_bytes=64)
+        grouped1 = ring.tile([P, JH, PACK], BF16, name="grouped1", tag="pass1", align_bytes=64)
+        picked1 = ring.tile([P, PACK, HEAD1], F32, name="picked1")
+
+        for i in range(PACK):
+            gather(picked0[:, i, :], 0, i, 0, HEAD0)
+        interleave(grouped0[:, :JH, :], picked0[:, :, :JH])
+        quantize_x(0, 0, grouped0[:, :JH, :])
+        split_on_vector(0, 0)
+        split_on_tensor(0, WK_COLS)
+        for n0 in range(0, N, WK_COLS):
+            split_on_tensor(1, n0)
+        for i in range(PACK):
+            width = HEAD1 if i < WIDE_PLANES else JH
+            gather(picked1[:, i, :width], 1, i, 0, width)
+        interleave(grouped1[:], picked1[:, :, :JH])
+        quantize_x(1, 0, grouped1[:])
+        interleave(grouped0[:, JH:HEAD0, :], picked0[:, :, JH:])
+
+        load_res(0, 0, 1)
         nc.sync.dma_start(wgt_tail[:], wgt[:, JH:])
         nc.sync.dma_start(wv_codes[:].bitcast(I32), wv_words.rearrange("a p n i -> p a (n i)").bitcast(I32))
-        for nt in range(NT):
-            load_res(nt, 0)
+        with nc.allow_non_contiguous_dma(reason="one bias value a partition and row tile"):
+            nc.sync.dma_start(bg_t[:], bg.rearrange("(c p) -> p c", p=P))
+        load_res(0, 1, NT)
+        load_res(1, 0, NT)
         nc.sync.dma_start(wgo_t[:], wgo)
-        for nt in range(NT):
-            load_res(nt, 1)
+        nc.sync.dma_start(offs2_t[:], offs2)
 
-        xq = {}
-
-        def gather(picked, a, j0, j1, weights):
+        def second_half_operands():
+            picked_tail = shared.tile([P, PACK, J - HEAD0], F32, name="picked_tail", offset=2048)
             for i in range(PACK):
-                nc.vector.tensor_tensor(
-                    picked[:, i, :], planes[a, i][:].indirect(offs_t[:, j0 // 16 : j1 // 16]), weights, ALU.mult
-                )
-
-        def quantize_x(a, jh, sources):
-            if (a, jh) == (1, 1):
-                grouped = shared.tile([P, JH, PACK], BF16, name="grouped_last", offset=8192, align_bytes=64)
-            else:
-                grouped = ring.tile(
-                    [P, JH, PACK], BF16, name=f"grouped_{a}_{jh}", tag="grouped", bufs=2, align_bytes=64
-                )
-            j0 = 0
-            for src in sources:
-                j1 = j0 + src.shape[2]
-                nc.scalar.copy(
-                    grouped[:, j0:j1, :].rearrange("p (c e) i -> p c i e", e=2),
-                    src.rearrange("p i (c e) -> p c i e", e=2),
-                )
-                j0 = j1
-            codes = keep.tile([P, JH], U32, name=f"x_codes_{a}_{jh}", align_bytes=64)
-            scales = keep.tile([P, JH], U8, name=f"x_scales_{a}_{jh}", align_bytes=64)
-            nc.vector.quantize_mx(
-                out=codes[:].bitcast(FP8X4), scales=scales[:], in_=grouped[:].rearrange("p j i -> p (j i)")
-            )
-            xq[a, jh] = (codes, scales)
-
-        for n0, n1 in ((0, 128), (128, 256), (256, 512)):
-            split_wk(0, n0, n1)
-        picked_head = keep.tile([P, PACK, EARLY], F32, name="picked_head")
-        gather(picked_head, 0, 0, EARLY, wgt_head[:])
-        quantize_x(0, 0, [picked_head[:, :, :JH]])
-        for n0, n1 in ((0, 256), (256, 512)):
-            split_wk(1, n0, n1)
-        picked = ring.tile([P, PACK, JH], F32, name="picked_1_0", tag="picked", bufs=1)
-        gather(picked, 1, 0, JH, wgt_head[:, :JH])
-        quantize_x(1, 0, [picked[:]])
-
-        def second_half():
-            picked_tail = shared.tile([P, PACK, J - EARLY], F32, name="picked_tail", offset=2048)
-            gather(picked_tail, 0, EARLY, J, wgt_tail[:, EARLY - JH :])
-            quantize_x(0, 1, [picked_head[:, :, JH:], picked_tail[:]])
-            picked_last = ring.tile([P, PACK, JH], F32, name="picked_1_1", tag="picked", bufs=1)
-            gather(picked_last, 1, JH, J, wgt_tail[:])
-            quantize_x(1, 1, [picked_last[:]])
-            for nt in range(2, NT):
-                w = ring.tile([P, T], F32, name=f"win{nt}", tag="plane1", bufs=PACK)
+                gather(picked_tail[:, i, :], 0, i, HEAD0, J)
+            interleave(grouped0[:, HEAD0:, :], picked_tail[:])
+            quantize_x(0, 1, grouped0[:, JH:, :])
+            grouped_last = shared.tile([P, JH, PACK], BF16, name="grouped_last", offset=9216, align_bytes=64)
+            for i in range(WIDE_PLANES, PACK):
+                gather(picked1[:, i, JH:], 1, i, JH, HEAD1)
+            interleave(grouped_last[:, : HEAD1 - JH, :], picked1[:, :, JH:])
+            picked_last = ring.tile([P, PACK, J - HEAD1], F32, name="picked_last", tag="pass1", align_bytes=64)
+            for i in range(PACK):
+                gather(picked_last[:, i, :], 1, i, HEAD1, J)
+            interleave(grouped_last[:, HEAD1 - JH :, :], picked_last[:])
+            quantize_x(1, 1, grouped_last[:])
+            for nt in range(NT // 2, NT):
+                window = ring.tile([P, T], F32, name=f"win{nt}", tag="plane1", bufs=PACK)
                 for c in range(0, T, JH):
-                    nc.gpsimd.memset(w[:, c : c + JH], 0.0)
-                windows.append(w)
+                    nc.gpsimd.memset(window[:, c : c + JH], 0.0)
+                windows.append(window)
 
         tiles = [(nt, jh) for jh in range(HALVES) for nt in range(NT)]
-        gate, veT, diff, neg_resT, neg_mixT, full = {}, {}, {}, {}, {}, {}
-        JB = JH // P
-        mixed = {}
-        on_tensor = tiles[1:7]
+        last = len(tiles) - 1
+        veT, neg_resT, gate, diff, mixed, neg_mixT, full = {}, {}, {}, {}, {}, {}, {}
 
-        def transpose_blocks(bank, sources):
-            for jb in range(JB):
-                cols = slice(jb * P, (jb + 1) * P)
-                for s, src in enumerate(sources):
-                    nc.tensor.matmul(
-                        bank[:, cols], src[:, cols], ident[:], is_transpose=True,
-                        start=(s == 0), stop=(s == len(sources) - 1),
-                    )
+        def on_plane(name, plane, slot):
+            return reuse.tile([P, JH], F32, name=name, offset=plane * PLANE_BYTES + slot * TILE_BYTES)
 
-        def turn_res(nt, jh):
-            bank = psum.tile([P, JH], F32, name=f"resT_ps_{nt}_{jh}", tag="resT", bufs=1)
-            transpose_blocks(bank, [res_t[nt, jh]])
-            if (nt, jh) == tiles[0]:
-                r = shared.tile([P, JH], F32, name="neg_resT_first", offset=0)
-            else:
-                r = ring.tile([P, JH], F32, name=f"neg_resT_{nt}_{jh}", tag="neg_resT", bufs=3)
-            nc.scalar.activation(r[:], bank[:], ACT.Copy, scale=-1.0)
-            neg_resT[nt, jh] = r
+        def turn_slot(name, k):
+            return ring.tile([P, JH], F32, name=name, tag=f"turn{k % TURN_SLOTS}")
 
-        def products(nt, jh):
+        def waits_for_next(k):
+            return k in SUM_ON_VECTOR[1:]
+
+        def values(k):
+            nt, jh = tiles[k]
             cols = slice(nt * P, (nt + 1) * P)
-            ve = psum.tile([P, JH], F32, name=f"veT_ps_{nt}_{jh}", tag="veT", bufs=1)
-            for jb in range(JB):
-                jcols = slice(jb * P, (jb + 1) * P)
+            bank = psum.tile([P, JH], F32, name=f"veT_ps_{k}", tag="veT")
+            for b in range(BLOCKS):
+                places = slice(b * P, (b + 1) * P)
                 for a in range(PASSES):
-                    xc, xs = xq[a, jh]
+                    x_codes, x_scales = xq[a, jh]
                     nc.tensor.matmul_mx(
-                        out=ve[:, jcols], lhsT=xc[:, jcols].bitcast(FP8X4), lhsT_scale=xs[:, jcols],
+                        out=bank[:, places], lhsT=x_codes[:, places].bitcast(FP8X4), lhsT_scale=x_scales[:, places],
                         rhs=wv_codes[:, a, cols].bitcast(FP8X4), rhs_scale=wv_sc[:, a, cols],
                         start=(a == 0), stop=(a == PASSES - 1),
                     )
-            if (nt, jh) == tiles[1]:
-                v = shared.tile([P, JH], F32, name="veT_second", offset=8192)
+            if k == 1:
+                veT[k] = shared.tile([P, JH], F32, name="veT_second", offset=8192)
             else:
-                v = ring.tile([P, JH], F32, name=f"veT_{nt}_{jh}", tag="veT_sb", bufs=3)
-            nc.scalar.copy(v[:], ve[:])
-            veT[nt, jh] = v
-            ke = psum.tile([P, JH], F32, name=f"ke_{nt}_{jh}", tag="ke", bufs=2)
+                veT[k] = turn_slot(f"veT_{k}", k)
+            nc.scalar.copy(veT[k][:], bank[:])
+
+        def turn_res(k):
+            nt, jh = tiles[k]
+            bank = psum.tile([P, JH], F32, name=f"resT_ps_{k}", tag="resT")
+            transpose_sum(bank, [blocks(res_half[jh][:, nt, :])])
+            if k == 0:
+                neg_resT[k] = shared.tile([P, JH], F32, name="neg_resT_first", offset=0)
+            else:
+                neg_resT[k] = ring.tile([P, JH], F32, name=f"neg_resT_{k}", tag="neg_resT", bufs=3)
+            nc.scalar.activation(neg_resT[k][:], bank[:], ACT.Copy, scale=-1.0)
+
+        def keys(k):
+            nt, jh = tiles[k]
+            bank = psum.tile([P, JH], F32, name=f"ke_{k}", tag="ke", bufs=2)
             steps = [(a, h) for a in range(PASSES) for h in range(2)]
             for s, (a, h) in enumerate(steps):
-                wc, ws = wk_q[a, nt][h]
-                xc, xs = xq[a, jh]
+                w_codes, w_scales = wk_q[a, nt][h]
+                x_codes, x_scales = xq[a, jh]
                 nc.tensor.matmul_mx(
-                    out=ke[:], lhsT=wc.bitcast(FP8X4), lhsT_scale=ws, rhs=xc[:].bitcast(FP8X4), rhs_scale=xs[:],
+                    out=bank[:], lhsT=w_codes.bitcast(FP8X4), lhsT_scale=w_scales,
+                    rhs=x_codes[:].bitcast(FP8X4), rhs_scale=x_scales[:],
                     start=(s == 0), stop=(s == len(steps) - 1),
                 )
-            if (nt, jh) == tiles[1]:
-                g = shared.tile([P, JH], F32, name="gate_second", offset=12288)
+            if waits_for_next(k - 1):
+                gate[k] = ring.tile([P, JH], F32, name=f"gate_{k}", tag=f"pair{k - 1}")
             else:
-                g = ring.tile([P, JH], F32, name=f"gate_{nt}_{jh}", tag="gate", bufs=3)
-            nc.scalar.activation(g[:], ke[:], ACT.Sigmoid, bias=bg_t[:, nt : nt + 1])
-            gate[nt, jh] = g
+                gate[k] = on_plane(f"gate_{k}", 0, k % GATE_SLOTS)
+            nc.scalar.activation(gate[k][:], bank[:], ACT.Sigmoid, bias=bg_t[:, nt : nt + 1])
 
-        def difference(nt, jh):
-            bank = psum.tile([P, JH], F32, name=f"diff_ps_{nt}_{jh}", tag="diff", bufs=2)
-            transpose_blocks(bank, [veT[nt, jh], neg_resT[nt, jh]])
-            diff[nt, jh] = bank
+        def difference(k):
+            diff[k] = psum.tile([P, JH], F32, name=f"diff_ps_{k}", tag="diff", bufs=2)
+            transpose_sum(diff[k], [blocks(veT[k]), blocks(neg_resT[k])])
 
-        def mix(nt, jh):
-            m = ring.tile([P, JH], F32, name=f"mixed_{nt}_{jh}", tag="mixed", bufs=2)
-            nc.vector.tensor_tensor(m[:], diff[nt, jh][:], gate[nt, jh][:], ALU.mult)
-            mixed[nt, jh] = m
-            if (nt, jh) not in on_tensor:
+        def mix(k):
+            mixed[k] = on_plane(f"mixed_{k}", 3, k % MIX_SLOTS)
+            nc.vector.tensor_tensor(mixed[k][:], diff[k][:], gate[k][:], ALU.mult)
+
+        def sum_on_tensor(k):
+            if k in SUM_ON_VECTOR:
                 return
-            bank = psum.tile([P, JH], F32, name=f"mixT_ps_{nt}_{jh}", tag="mixT", bufs=1)
-            transpose_blocks(bank, [m])
-            mt = ring.tile([P, JH], F32, name=f"neg_mixT_{nt}_{jh}", tag="neg_mixT", bufs=2)
-            nc.scalar.activation(mt[:], bank[:], ACT.Copy, scale=-1.0)
-            neg_mixT[nt, jh] = mt
+            turned = psum.tile([P, JH], F32, name=f"mixT_ps_{k}", tag="mixT")
+            transpose_sum(turned, [blocks(mixed[k])])
+            if k < last:
+                neg_mixT[k] = turn_slot(f"neg_mixT_{k}", k + 1)
+            else:
+                neg_mixT[k] = ring.tile([P, JH], F32, name=f"neg_mixT_{k}", tag="spare", bufs=2)
+            nc.scalar.activation(neg_mixT[k][:], turned[:], ACT.Copy, scale=-1.0)
+            bank = psum.tile([P, JH], F32, name=f"full_ps_{k}", tag="full")
+            transpose_sum(bank, [blocks(neg_mixT[k]), blocks(neg_resT[k])])
+            full[k] = on_plane(f"full_{k}", 2, k % MIX_SLOTS)
+            nc.scalar.activation(full[k][:], bank[:], ACT.Copy, scale=-1.0)
 
-        def add_res(nt, jh):
-            if (nt, jh) not in on_tensor:
-                if (nt, jh) == tiles[0]:
-                    f = shared.tile([P, JH], F32, name="full_first", offset=12288)
-                else:
-                    f = ring.tile([P, JH], F32, name=f"full_{nt}_{jh}", tag="full_sb", bufs=3)
-                nc.vector.tensor_tensor(f[:], mixed[nt, jh][:], res_t[nt, jh][:], ALU.add)
-                full[nt, jh] = f
+        def sum_on_vector(k):
+            if k not in SUM_ON_VECTOR:
                 return
-            bank = psum.tile([P, JH], F32, name=f"full_ps_{nt}_{jh}", tag="full", bufs=1)
-            transpose_blocks(bank, [neg_mixT[nt, jh], neg_resT[nt, jh]])
-            f = ring.tile([P, JH], F32, name=f"full_{nt}_{jh}", tag="full_sb", bufs=3)
-            nc.scalar.activation(f[:], bank[:], ACT.Copy, scale=-1.0)
-            full[nt, jh] = f
+            nt, jh = tiles[k]
+            if waits_for_next(k):
+                full[k] = ring.tile([P, JH], F32, name=f"full_{k}", tag=f"pair{k}")
+            else:
+                full[k] = on_plane(f"full_{k}", 2, k % MIX_SLOTS)
+            nc.vector.tensor_tensor(full[k][:], mixed[k][:], res_half[jh][:, nt, :], ALU.add)
 
-        def scatter(nt, jh):
-            lst = offs2_t[:, jh * LIST_COLS : (jh + 1) * LIST_COLS]
+        def scatter(k):
+            nt, jh = tiles[k]
+            places = offs2_t[:, jh * JH // GROUP : (jh + 1) * JH // GROUP]
             nc.vector.tensor_tensor(
-                windows[nt][:].indirect(lst), full[nt, jh][:], wgo_t[:, jh * JH : (jh + 1) * JH], ALU.mult
+                windows[nt][:].indirect(places), full[k][:], wgo_t[:, jh * JH : (jh + 1) * JH], ALU.mult
             )
             if jh == HALVES - 1:
                 nc.sync.dma_start(out[nt * P : (nt + 1) * P, :], windows[nt][:])
 
-        stages = [(mix, 0), (difference, -1), (add_res, 0), (scatter, 1), (turn_res, -2), (products, -2)]
-        for step in range(-2, len(tiles) + 1):
-            for stage, lag in stages:
-                if stage is products and step == 1:
-                    second_half()
-                if stage is add_res and step == 0:
-                    continue
-                if stage is add_res and step == 1:
-                    add_res(*tiles[0])
-                if 0 <= step - lag < len(tiles):
-                    stage(*tiles[step - lag])
+        stages = [
+            (values, AHEAD), (difference, 1), (mix, 0), (sum_on_tensor, 0), (sum_on_vector, -1),
+            (turn_res, AHEAD), (keys, AHEAD), (scatter, -1),
+        ]
+        for step in range(-AHEAD, len(tiles) + 1):
+            for stage, shift in stages:
+                if 0 <= step + shift <= last:
+                    stage(step + shift)
+            if step + AHEAD == NT - 1:
+                second_half_operands()

from contextlib import ExitStack

import concourse.mybir as mybir
from concourse.masks import make_identity

K, N, T, J = 1024, 512, 2048, 1024
FLOPS = 3 * 2 * K * N * J

F32 = mybir.dt.float32
BF16 = mybir.dt.bfloat16
I32 = mybir.dt.int32
U32 = mybir.dt.uint32
U16 = mybir.dt.uint16
U8 = mybir.dt.uint8
FP8X4 = mybir.dt.float8_e4m3fn_x4
ALU = mybir.AluOpType
ACT = mybir.ActivationFunctionType

P = 128
PACK = 4
PASSES = K // (P * PACK)
GROUP = 16
JH = 512
HALVES = J // JH
NT = N // P
BLOCKS = JH // P
TILE_BYTES = JH * 4
PLANE_BYTES = T * 4

HI_MASK = 0xFFF00000 - (1 << 32)
PAIR_MASK = 0xFFF0FFF0 - (1 << 32)
SIGN_BIT = -(1 << 31)

WK_COLS = 256
HEAD0 = 896
HEAD1 = 640
WIDE_PLANES = 2
SUM_ON_VECTOR = (0, 1, 3)
AHEAD = 2
TURN_SLOTS = 4
GATE_SLOTS = 3
MIX_SLOTS = 4


def tile_list_hl_hwayS_kernel(
    tc, xT, wgt, wk, wv_words, wv_scales, bg, res, wgo, offs, offs2, out
):
    nc = tc.nc
    with ExitStack() as ctx:
        keep = ctx.enter_context(tc.tile_pool(name="keep", bufs=1))
        ring = ctx.enter_context(tc.tile_pool(name="ring", bufs=1))
        shared = ctx.enter_context(tc.tile_pool(name="shared", bufs=1))
        reuse = ctx.enter_context(tc.tile_pool(name="reuse", bufs=1))
        psum = ctx.enter_context(tc.psum_pool(name="psum", bufs=1))

        offs_t = keep.tile([P, J // GROUP], U16, name="offs_t")
        offs2_t = keep.tile([P, J // GROUP], U16, name="offs2_t")
        wgt_head = shared.tile([P, HEAD0], F32, name="wgt_head", offset=1024)
        wgt_tail = keep.tile([P, JH], F32, name="wgt_tail")
        wgo_t = keep.tile([P, J], F32, name="wgo_t")
        bg_t = keep.tile([P, NT], F32, name="bg_t")
        wv_codes = keep.tile([P, PASSES, N], U32, name="wv_codes", align_bytes=64)
        wv_sc = keep.tile([P, PASSES, N], U8, name="wv_sc", align_bytes=64)

        x_rows = xT.rearrange("(a p i) t -> a i p t", a=PASSES, i=PACK)
        wk_rows = wk.rearrange("(a p i) n -> a p i n", a=PASSES, i=PACK)
        res_rows = res.rearrange("(c p) j -> p c j", p=P)

        ident = keep.tile([P, P], F32, name="ident")
        make_identity(nc, ident[:])
        nc.vector.memset(wv_sc[:].bitcast(I32), 0)
        windows = []
        for nt in range(NT // 2):
            window = keep.tile([P, T], F32, name=f"win{nt}")
            nc.vector.memset(window[:].bitcast(I32), 0)
            windows.append(window)

        wk_raw, planes, res_half = {}, {}, {}
        wk_q, xq = {}, {}

        def load_wk(a):
            wk_raw[a] = ring.tile([P, PACK, N], F32, name=f"wk_raw_{a}", tag="wk_raw", bufs=PASSES)
            nc.sync.dma_start(wk_raw[a][:], wk_rows[a])

        def load_plane(a, i):
            if a == 0:
                plane = reuse.tile([P, T], F32, name=f"plane_{a}_{i}", offset=i * PLANE_BYTES)
            else:
                plane = ring.tile([P, T], F32, name=f"plane_{a}_{i}", tag="plane1", bufs=PACK)
            nc.sync.dma_start(plane[:], x_rows[a, i])
            planes[a, i] = plane

        def load_res(jh, nt0, nt1):
            if nt0 == 0:
                res_half[jh] = ring.tile([P, NT, JH], F32, name=f"res_{jh}", tag="wk_raw", bufs=PASSES)
            nc.sync.dma_start(res_half[jh][:, nt0:nt1, :], res_rows[:, nt0:nt1, jh * JH : (jh + 1) * JH])

        def transpose_sum(bank, sources):
            for b in range(BLOCKS):
                for s, source in enumerate(sources):
                    nc.tensor.matmul(
                        bank[:, b * P : (b + 1) * P], source(b), ident[:], is_transpose=True,
                        start=(s == 0), stop=(s == len(sources) - 1),
                    )

        def blocks(t):
            return lambda b: t[:, b * P : (b + 1) * P]

        def by_plane(ap):
            return ap.rearrange("p i (c e) -> p c i e", e=2)

        def by_column(ap):
            return ap.rearrange("p (c e) i -> p c i e", e=2)

        def quantize_wk(a, n0, part):
            width = part[:].shape[2]
            codes = keep.tile([P, 2, width], U32, name=f"wk_codes_{a}_{n0}", align_bytes=64)
            scales = keep.tile([P, 2, width], U8, name=f"wk_scales_{a}_{n0}", align_bytes=64)
            nc.vector.quantize_mx(
                out=codes[:].rearrange("p h n -> p (h n)").bitcast(FP8X4),
                scales=scales[:].rearrange("p h n -> p (h n)"),
                in_=part[:].rearrange("p h n i -> p (h n i)"),
            )
            for c in range(0, width, P):
                wk_q[a, (n0 + c) // P] = [(codes[:, h, c : c + P], scales[:, h, c : c + P]) for h in range(2)]

        def split_on_tensor(a, n0):
            raw = wk_raw[a]
            neg_hi = ring.tile([P, PACK, WK_COLS], F32, name=f"neg_hi_{a}_{n0}", tag="neg_hi", bufs=2)
            part = ring.tile(
                [P, 2, WK_COLS, PACK], BF16, name=f"wk_parts_{a}_{n0}", tag="wk_parts", bufs=2, align_bytes=64
            )
            nc.vector.tensor_scalar(
                neg_hi[:].bitcast(I32), raw[:, :, n0 : n0 + WK_COLS].bitcast(I32),
                HI_MASK, SIGN_BIT, ALU.bitwise_and, ALU.bitwise_xor,
            )
            for c in range(0, WK_COLS, P):
                turned = psum.tile([P, JH], F32, name=f"loT_ps_{a}_{n0 + c}", tag="diff", bufs=2)
                transpose_sum(turned, [lambda i: raw[:, i, n0 + c : n0 + c + P], lambda i: neg_hi[:, i, c : c + P]])
                lo_t = ring.tile([P, JH], F32, name=f"loT_{a}_{n0 + c}", tag="spare", bufs=2)
                nc.scalar.copy(lo_t[:], turned[:])
                back = psum.tile([P, JH], F32, name=f"lo_ps_{a}_{n0 + c}", tag="full")
                transpose_sum(back, [blocks(lo_t)])
                nc.scalar.copy(part[:, 1, c : c + P, :], back[:].rearrange("p (i n) -> p n i", i=PACK))
            nc.scalar.activation(by_column(part[:, 0, :, :]), by_plane(neg_hi[:]), ACT.Copy, scale=-1.0)
            quantize_wk(a, n0, part)

        def split_on_vector(a, n0):
            starts = range(n0, n0 + WK_COLS, P)
            raws = [wk_raw[a][:, :, c : c + P] for c in starts]
            parts = []
            for c, raw in zip(starts, raws):
                part = ring.tile(
                    [P, 2, P, PACK], BF16, name=f"wk_parts_{a}_{c}", tag="wk_parts_v", bufs=2, align_bytes=64
                )
                halves = raw.bitcast(BF16).rearrange("p i (c e h) -> p c i e h", e=2, h=2)
                nc.scalar.copy(by_column(part[:, 0, :, :]), halves[:, :, :, :, 1])
                parts.append(part)

            def mask(part):
                pairs = part[:, 0, :, :].rearrange("p n i -> p (n i)").bitcast(I32)
                nc.vector.tensor_scalar(pairs, pairs, PAIR_MASK, None, ALU.bitwise_and)

            mask(parts[0])
            for u, part in enumerate(parts):
                nc.vector.tensor_tensor(
                    by_column(part[:, 1, :, :]), by_plane(raws[u]), by_column(part[:, 0, :, :]), ALU.subtract
                )
                if u + 1 < len(parts):
                    mask(parts[u + 1])
                quantize_wk(a, starts[u], part)

        def gather(dst, a, i, j0, j1):
            weights = wgt_head[:, j0:j1] if j0 == 0 else wgt_tail[:, j0 - JH : j1 - JH]
            nc.vector.tensor_tensor(
                dst, planes[a, i][:].indirect(offs_t[:, j0 // GROUP : j1 // GROUP]), weights, ALU.mult
            )

        def interleave(grouped, picked):
            nc.scalar.copy(by_column(grouped), by_plane(picked))

        def quantize_x(a, jh, grouped):
            codes = keep.tile([P, JH], U32, name=f"x_codes_{a}_{jh}", align_bytes=64)
            scales = keep.tile([P, JH], U8, name=f"x_scales_{a}_{jh}", align_bytes=64)
            nc.vector.quantize_mx(
                out=codes[:].bitcast(FP8X4), scales=scales[:], in_=grouped.rearrange("p j i -> p (j i)")
            )
            xq[a, jh] = (codes, scales)

        load_wk(0)
        nc.sync.dma_start(offs_t[:], offs)
        load_wk(1)
        nc.sync.dma_start(wgt_head[:], wgt[:, :HEAD0])
        plane_order = [(a, i) for a in range(PASSES) for i in range(PACK)]
        for a, i in plane_order[:-1]:
            load_plane(a, i)
        for q in range(4):
            nc.sync.dma_start(
                wv_sc[32 * q : 32 * q + 4, :, :].bitcast(I32),
                wv_scales[:, 4 * q : 4 * q + 4, :].rearrange("a r n -> r a n").bitcast(I32),
            )
        load_plane(*plane_order[-1])

        picked0 = keep.tile([P, PACK, HEAD0], F32, name="picked0")
        grouped0 = keep.tile([P, J, PACK], BF16, name="grouped0", align_bytes=64)
        grouped1 = ring.tile([P, JH, PACK], BF16, name="grouped1", tag="pass1", align_bytes=64)
        picked1 = ring.tile([P, PACK, HEAD1], F32, name="picked1")

        for i in range(PACK):
            gather(picked0[:, i, :], 0, i, 0, HEAD0)
        interleave(grouped0[:, :JH, :], picked0[:, :, :JH])
        quantize_x(0, 0, grouped0[:, :JH, :])
        split_on_vector(0, 0)
        split_on_tensor(0, WK_COLS)
        for n0 in range(0, N, WK_COLS):
            split_on_tensor(1, n0)
        for i in range(PACK):
            width = HEAD1 if i < WIDE_PLANES else JH
            gather(picked1[:, i, :width], 1, i, 0, width)
        interleave(grouped1[:], picked1[:, :, :JH])
        quantize_x(1, 0, grouped1[:])
        interleave(grouped0[:, JH:HEAD0, :], picked0[:, :, JH:])

        load_res(0, 0, 1)
        nc.sync.dma_start(wgt_tail[:], wgt[:, JH:])
        nc.sync.dma_start(wv_codes[:].bitcast(I32), wv_words.rearrange("a p n i -> p a (n i)").bitcast(I32))
        with nc.allow_non_contiguous_dma(reason="one bias value a partition and row tile"):
            nc.sync.dma_start(bg_t[:], bg.rearrange("(c p) -> p c", p=P))
        load_res(0, 1, NT)
        load_res(1, 0, NT)
        nc.sync.dma_start(wgo_t[:], wgo)
        nc.sync.dma_start(offs2_t[:], offs2)

        def second_half_operands():
            picked_tail = shared.tile([P, PACK, J - HEAD0], F32, name="picked_tail", offset=2048)
            for i in range(PACK):
                gather(picked_tail[:, i, :], 0, i, HEAD0, J)
            interleave(grouped0[:, HEAD0:, :], picked_tail[:])
            quantize_x(0, 1, grouped0[:, JH:, :])
            grouped_last = shared.tile([P, JH, PACK], BF16, name="grouped_last", offset=9216, align_bytes=64)
            for i in range(WIDE_PLANES, PACK):
                gather(picked1[:, i, JH:], 1, i, JH, HEAD1)
            interleave(grouped_last[:, : HEAD1 - JH, :], picked1[:, :, JH:])
            picked_last = ring.tile([P, PACK, J - HEAD1], F32, name="picked_last", tag="pass1", align_bytes=64)
            for i in range(PACK):
                gather(picked_last[:, i, :], 1, i, HEAD1, J)
            interleave(grouped_last[:, HEAD1 - JH :, :], picked_last[:])
            quantize_x(1, 1, grouped_last[:])
            for nt in range(NT // 2, NT):
                window = ring.tile([P, T], F32, name=f"win{nt}", tag="plane1", bufs=PACK)
                for c in range(0, T, JH):
                    nc.gpsimd.memset(window[:, c : c + JH], 0.0)
                windows.append(window)

        tiles = [(nt, jh) for jh in range(HALVES) for nt in range(NT)]
        last = len(tiles) - 1
        veT, neg_resT, gate, diff, mixed, neg_mixT, full = {}, {}, {}, {}, {}, {}, {}

        def on_plane(name, plane, slot):
            return reuse.tile([P, JH], F32, name=name, offset=plane * PLANE_BYTES + slot * TILE_BYTES)

        def turn_slot(name, k):
            return ring.tile([P, JH], F32, name=name, tag=f"turn{k % TURN_SLOTS}")

        def waits_for_next(k):
            return k in SUM_ON_VECTOR[1:]

        def values(k):
            nt, jh = tiles[k]
            cols = slice(nt * P, (nt + 1) * P)
            bank = psum.tile([P, JH], F32, name=f"veT_ps_{k}", tag="veT")
            for b in range(BLOCKS):
                places = slice(b * P, (b + 1) * P)
                for a in range(PASSES):
                    x_codes, x_scales = xq[a, jh]
                    nc.tensor.matmul_mx(
                        out=bank[:, places], lhsT=x_codes[:, places].bitcast(FP8X4), lhsT_scale=x_scales[:, places],
                        rhs=wv_codes[:, a, cols].bitcast(FP8X4), rhs_scale=wv_sc[:, a, cols],
                        start=(a == 0), stop=(a == PASSES - 1),
                    )
            if k == 1:
                veT[k] = shared.tile([P, JH], F32, name="veT_second", offset=8192)
            else:
                veT[k] = turn_slot(f"veT_{k}", k)
            nc.scalar.copy(veT[k][:], bank[:])

        def turn_res(k):
            nt, jh = tiles[k]
            bank = psum.tile([P, JH], F32, name=f"resT_ps_{k}", tag="resT")
            transpose_sum(bank, [blocks(res_half[jh][:, nt, :])])
            if k == 0:
                neg_resT[k] = shared.tile([P, JH], F32, name="neg_resT_first", offset=0)
            else:
                neg_resT[k] = ring.tile([P, JH], F32, name=f"neg_resT_{k}", tag="neg_resT", bufs=3)
            nc.scalar.activation(neg_resT[k][:], bank[:], ACT.Copy, scale=-1.0)

        def keys(k):
            nt, jh = tiles[k]
            bank = psum.tile([P, JH], F32, name=f"ke_{k}", tag="ke", bufs=2)
            steps = [(a, h) for a in range(PASSES) for h in range(2)]
            for s, (a, h) in enumerate(steps):
                w_codes, w_scales = wk_q[a, nt][h]
                x_codes, x_scales = xq[a, jh]
                nc.tensor.matmul_mx(
                    out=bank[:], lhsT=w_codes.bitcast(FP8X4), lhsT_scale=w_scales,
                    rhs=x_codes[:].bitcast(FP8X4), rhs_scale=x_scales[:],
                    start=(s == 0), stop=(s == len(steps) - 1),
                )
            if waits_for_next(k - 1):
                gate[k] = ring.tile([P, JH], F32, name=f"gate_{k}", tag=f"pair{k - 1}")
            else:
                gate[k] = on_plane(f"gate_{k}", 0, k % GATE_SLOTS)
            nc.scalar.activation(gate[k][:], bank[:], ACT.Sigmoid, bias=bg_t[:, nt : nt + 1])

        def difference(k):
            diff[k] = psum.tile([P, JH], F32, name=f"diff_ps_{k}", tag="diff", bufs=2)
            transpose_sum(diff[k], [blocks(veT[k]), blocks(neg_resT[k])])

        def mix(k):
            mixed[k] = on_plane(f"mixed_{k}", 3, k % MIX_SLOTS)
            nc.vector.tensor_tensor(mixed[k][:], diff[k][:], gate[k][:], ALU.mult)

        def sum_on_tensor(k):
            if k in SUM_ON_VECTOR:
                return
            turned = psum.tile([P, JH], F32, name=f"mixT_ps_{k}", tag="mixT")
            transpose_sum(turned, [blocks(mixed[k])])
            if k < last:
                neg_mixT[k] = turn_slot(f"neg_mixT_{k}", k + 1)
            else:
                neg_mixT[k] = ring.tile([P, JH], F32, name=f"neg_mixT_{k}", tag="spare", bufs=2)
            nc.scalar.activation(neg_mixT[k][:], turned[:], ACT.Copy, scale=-1.0)
            bank = psum.tile([P, JH], F32, name=f"full_ps_{k}", tag="full")
            transpose_sum(bank, [blocks(neg_mixT[k]), blocks(neg_resT[k])])
            full[k] = on_plane(f"full_{k}", 2, k % MIX_SLOTS)
            nc.scalar.activation(full[k][:], bank[:], ACT.Copy, scale=-1.0)

        def sum_on_vector(k):
            if k not in SUM_ON_VECTOR:
                return
            nt, jh = tiles[k]
            if waits_for_next(k):
                full[k] = ring.tile([P, JH], F32, name=f"full_{k}", tag=f"pair{k}")
            else:
                full[k] = on_plane(f"full_{k}", 2, k % MIX_SLOTS)
            nc.vector.tensor_tensor(full[k][:], mixed[k][:], res_half[jh][:, nt, :], ALU.add)

        def scatter(k):
            nt, jh = tiles[k]
            places = offs2_t[:, jh * JH // GROUP : (jh + 1) * JH // GROUP]
            nc.vector.tensor_tensor(
                windows[nt][:].indirect(places), full[k][:], wgo_t[:, jh * JH : (jh + 1) * JH], ALU.mult
            )
            if jh == HALVES - 1:
                nc.sync.dma_start(out[nt * P : (nt + 1) * P, :], windows[nt][:])

        stages = [
            (values, AHEAD), (difference, 1), (mix, 0), (sum_on_tensor, 0), (sum_on_vector, -1),
            (turn_res, AHEAD), (keys, AHEAD), (scatter, -1),
        ]
        for step in range(-AHEAD, len(tiles) + 1):
            for stage, shift in stages:
                if 0 <= step + shift <= last:
                    stage(step + shift)
            if step + AHEAD == NT - 1:
                second_half_operands()
